import numpy as np
import ml_dtypes


def mxq(x, axis, fmt="e4m3"):
    dtype, down = {"e4m3": (ml_dtypes.float8_e4m3fn, 7), "e5m2": (ml_dtypes.float8_e5m2, 14)}[fmt]
    v = np.moveaxis(np.asarray(x, np.float32).astype(ml_dtypes.bfloat16).astype(np.float64), axis, -1)
    blocks = v.reshape(v.shape[:-1] + (-1, 32))
    amax = np.abs(blocks).max(-1, keepdims=True)
    byte = np.maximum(np.where(amax > 0, np.frexp(amax)[1] - 1 + 127, 0) - down, 1)
    scale = np.exp2(byte - 127.0)
    codes = (blocks / scale).astype(np.float32).astype(dtype).astype(np.float64)
    return np.moveaxis((codes * scale).reshape(v.shape), -1, axis)


WIDE = False


def mx_kscale(k):
    if not WIDE:
        return np.ones(k)
    levels = np.array([10, -10, 5, -5, 0])
    if k % 512:
        return np.exp2(np.random.permutation(np.resize(levels, k // 32))).repeat(32)
    a = np.empty((k // 512, 16))
    for p in range(k // 512):
        a[p, :8] = np.random.permutation(np.resize(levels, 8))
        for g in range(8):
            far = levels[np.abs(levels - a[p, g]) >= 10]
            a[p, g + 8] = far[np.random.randint(len(far))]
    return np.exp2(a.ravel()).repeat(32)


def f64(x):
    return np.asarray(x).astype(np.float64)


def striped(idx):
    return np.tile(idx.reshape(-1, 16).T, (8, 1)).astype(np.uint16)


def unstriped(offs):
    return offs[:16].T.reshape(-1).astype(np.int64)


def pack_weight(w):
    k, n = w.shape
    w = f64(np.asarray(w, np.float32).astype(ml_dtypes.bfloat16)).reshape(k // 32, 32, n)
    amax = np.abs(w).max(1)
    byte = np.clip(np.where(amax > 0, np.frexp(amax)[1] - 1 + 127 - 7, 1), 1, 254)
    scaled = (w * np.exp2(127.0 - byte)[:, None, :]).reshape(k, n).astype(np.float32)
    words = np.ascontiguousarray(scaled.reshape(k // 512, 128, 4, n).transpose(0, 1, 3, 2)).astype(ml_dtypes.float8_e4m3fn).view(np.uint8)
    return words, np.ascontiguousarray(byte.astype(np.uint8).reshape(k // 512, 16, n))


def unpack_weight(words, scales):
    g, p, n, _ = words.shape
    vals = np.ascontiguousarray(words).view(ml_dtypes.float8_e4m3fn).astype(np.float64) * np.repeat(np.exp2(scales.astype(np.float64) - 127.0), 8, axis=1)[..., None]
    return vals.transpose(0, 1, 3, 2).reshape(g * 512, n)


def relu(v):
    return np.maximum(v, 0.0)


K, T, S, V, N = 512, 4096, 1024, 512, 128


def setup_inputs():
    n = np.random.standard_normal
    s = mx_kscale(K)[:, None]
    packed_xT = pack_weight(n((K, T)) * s)
    packed_w1 = pack_weight(n((K, N)) / np.sqrt(K) / s)
    packed_w2 = pack_weight(n((K, N)) / np.sqrt(K) / s)
    return {
        "x_words": packed_xT[0],
        "x_scales": packed_xT[1],
        "sT": (n((K, V)) * s).astype(np.float32),
        "w1_words": packed_w1[0],
        "w1_scales": packed_w1[1],
        "w2_words": packed_w2[0],
        "w2_scales": packed_w2[1],
        "offs": striped(np.random.permutation(T)[:S]),
        "par": striped(np.random.randint(0, V, S)),
    }


def reference(x_words, x_scales, sT, w1_words, w1_scales, w2_words, w2_scales, offs, par):
    xq = unpack_weight(x_words, x_scales)[:, unstriped(offs)]
    y = unpack_weight(w1_words, w1_scales).T @ xq
    t = unpack_weight(w2_words, w2_scales).T @ mxq(f64(sT), 0, "e4m3")
    return relu(y + t[:, unstriped(par)])

@@ -1,0 +1,125 @@
+from contextlib import ExitStack
+
+import concourse.mybir as mybir
+
+K, T, S, V, N = 512, 4096, 1024, 512, 128
+FLOPS = 2 * K * N * (S + V)
+
+F32 = mybir.dt.float32
+BF16 = mybir.dt.bfloat16
+I32 = mybir.dt.int32
+U32 = mybir.dt.uint32
+U16 = mybir.dt.uint16
+U8 = mybir.dt.uint8
+FP8X4 = mybir.dt.float8_e4m3fn_x4
+ADD = mybir.AluOpType.add
+RELU = mybir.ActivationFunctionType.Relu
+
+P = 128
+PACK = 4
+STRIPE = 16
+HALF = S // 2
+SCALAR_COLS = 192
+ROW0 = P - 16
+
+
+def words_of(packed):
+    return packed[0].rearrange("p n t -> p (n t)").bitcast(I32)
+
+
+def tile_picked_fpn_relu_p_kernel(
+    tc, x_words, x_scales, sT, w1_words, w1_scales, w2_words, w2_scales, offs, par, out
+):
+    nc = tc.nc
+    with ExitStack() as ctx:
+        keep = ctx.enter_context(tc.tile_pool(name="keep", bufs=1))
+        psum = ctx.enter_context(tc.psum_pool(name="psum", bufs=1))
+
+        offs_sb = keep.tile([P, S // STRIPE], U16, name="offs_sb")
+        par_sb = keep.tile([P, S // STRIPE], U16, name="par_sb")
+        xs_table = keep.tile([P, T], U8, name="xs_table", align_bytes=64)
+        xw_table = keep.tile([P, T], U32, name="xw_table", align_bytes=64)
+        s_raw = keep.tile([P, PACK, V], F32, name="s_raw", align_bytes=64)
+        w1_codes = keep.tile([P, N], U32, name="w1_codes", align_bytes=64)
+        w2_codes = keep.tile([P, N], U32, name="w2_codes", align_bytes=64)
+        w1_plane = keep.tile([P, N], U8, name="w1_plane", align_bytes=64)
+        w2_plane = keep.tile([P, N], U8, name="w2_plane", align_bytes=64)
+        xs_plane = keep.tile([P, S], U8, name="xs_plane", align_bytes=64)
+
+        nc.vector.memset(xs_table[0:ROW0, :].bitcast(I32), 0)
+        nc.gpsimd.memset(w2_plane[:].bitcast(I32), 0)
+        nc.gpsimd.memset(w1_plane[:].bitcast(I32), 0)
+        nc.gpsimd.memset(xs_plane[:].bitcast(I32), 0)
+
+        warm = keep.tile([P, 2], F32, name="warm")
+        nc.gpsimd.memset(warm[:, 0:1], 0.0)
+        nc.scalar.activation(warm[:, 1:2], warm[:, 0:1], RELU)
+
+        def load_plane(queue, plane, rows):
+            for q in range(4):
+                queue.dma_start(plane[32 * q : 32 * q + 4, :].bitcast(I32), rows[0, 4 * q : 4 * q + 4, :].bitcast(I32))
+
+        nc.sync.dma_start(offs_sb[:], offs)
+        nc.sync.dma_start(xs_table[ROW0:P, :].bitcast(I32), x_scales[0].bitcast(I32))
+        nc.sync.dma_start(s_raw[:], sT.rearrange("(p j) v -> p j v", j=PACK))
+        nc.sync.dma_start(w2_codes[:].bitcast(I32), words_of(w2_words))
+        load_plane(nc.sync, w2_plane, w2_scales)
+        nc.sync.dma_start(par_sb[:], par)
+        nc.sync.dma_start(xw_table[:].bitcast(I32), words_of(x_words))
+        nc.sync.dma_start(w1_codes[:].bitcast(I32), words_of(w1_words))
+        load_plane(nc.gpsimd, w1_plane, w1_scales)
+
+        def entries(lst, a, b):
+            return lst[:, a // STRIPE : b // STRIPE]
+
+        xs_picked = keep.tile([P, S], U8, name="xs_picked", align_bytes=64)
+        nc.vector.tensor_copy(xs_picked[:, 0:HALF], xs_table[:].indirect(entries(offs_sb, 0, HALF)))
+
+        s_grouped = keep.tile([P, V * PACK], BF16, name="s_grouped", align_bytes=64)
+
+        def interleave(copy, a, b):
+            copy(
+                s_grouped[:, PACK * a : PACK * b].rearrange("p (c i t) -> p c t i", i=4, t=PACK),
+                s_raw[:, :, a:b].rearrange("p t (c i) -> p c t i", i=4),
+            )
+
+        interleave(nc.scalar.copy, 0, SCALAR_COLS)
+        interleave(nc.vector.tensor_copy, V // 2, V)
+        interleave(nc.vector.tensor_copy, SCALAR_COLS, V // 2)
+
+        t_table = keep.tile([P, V], F32, name="t_table", align_bytes=64)
+        for h in (1, 0):
+            cols = slice(h * V // 2, (h + 1) * V // 2)
+            s_codes = keep.tile([P, V // 2], U32, name="s_codes%d" % h, align_bytes=64)
+            s_plane = keep.tile([P, V // 2], U8, name="s_plane%d" % h, align_bytes=64)
+            nc.vector.quantize_mx(s_codes[:].bitcast(FP8X4), s_plane[:], s_grouped[:, PACK * cols.start : PACK * cols.stop])
+            t_bank = psum.tile([P, V // 2], F32, name="t_bank%d" % h)
+            nc.tensor.matmul_mx(t_bank[:], lhsT=w2_codes[:].bitcast(FP8X4), lhsT_scale=w2_plane[:],
+                                rhs=s_codes[:].bitcast(FP8X4), rhs_scale=s_plane[:], start=True, stop=True)
+            nc.scalar.copy(t_table[:, cols], t_bank[:])
+
+        nc.vector.tensor_copy(xs_picked[:, HALF:S], xs_table[:].indirect(entries(offs_sb, HALF, S)))
+        for r in range(4):
+            nc.sync.dma_start(xs_plane[32 * r : 32 * r + 4, :].bitcast(I32), xs_picked[ROW0 + 4 * r : ROW0 + 4 * r + 4, :].bitcast(I32))
+
+        t_picked = keep.tile([P, S], F32, name="t_picked", align_bytes=64)
+        for a in range(0, S, 256):
+            nc.vector.tensor_copy(t_picked[:, a : a + 256], t_table[:].indirect(entries(par_sb, a, a + 256)))
+
+        xw_picked = []
+        for h in range(2):
+            picked = keep.tile([P, HALF], U32, name="xw_picked%d" % h, align_bytes=64)
+            nc.vector.tensor_copy(picked[:], xw_table[:].indirect(entries(offs_sb, h * HALF, (h + 1) * HALF)))
+            xw_picked.append(picked)
+
+        for a, b in ((0, 512), (512, 768), (768, 1024)):
+            h = a // HALF
+            y_bank = psum.tile([P, b - a], F32, name="y_bank%d" % a)
+            nc.tensor.matmul_mx(y_bank[:], lhsT=w1_codes[:].bitcast(FP8X4), lhsT_scale=w1_plane[:],
+                                rhs=xw_picked[h][:, a - h * HALF : b - h * HALF].bitcast(FP8X4),
+                                rhs_scale=xs_plane[:, a:b], start=True, stop=True)
+            total = keep.tile([P, b - a], F32, name="total%d" % a, align_bytes=64)
+            nc.vector.tensor_tensor(total[:], y_bank[:], t_picked[:, a:b], ADD)
+            result = keep.tile([P, b - a], F32, name="result%d" % a, align_bytes=64)
+            nc.scalar.activation(result[:], total[:], RELU)
+            nc.sync.dma_start(out[:, a:b], result[:])

@@ -19,7 +19,7 @@ P = 128
 PACK = 4
 STRIPE = 16
 HALF = S // 2
-SCALAR_COLS = 192
+SCALAR_COLS = 224
 ROW0 = P - 16
 
 
@@ -55,19 +55,20 @@ def tile_picked_fpn_relu_p_kernel(
         nc.gpsimd.memset(warm[:, 0:1], 0.0)
         nc.scalar.activation(warm[:, 1:2], warm[:, 0:1], RELU)
 
-        def load_plane(queue, plane, rows):
-            for q in range(4):
+        def load_plane(queue, plane, rows, quadrants):
+            for q in quadrants:
                 queue.dma_start(plane[32 * q : 32 * q + 4, :].bitcast(I32), rows[0, 4 * q : 4 * q + 4, :].bitcast(I32))
 
+        load_plane(nc.gpsimd, w1_plane, w1_scales, range(2, 4))
         nc.sync.dma_start(offs_sb[:], offs)
+        nc.sync.dma_start(par_sb[:], par)
         nc.sync.dma_start(xs_table[ROW0:P, :].bitcast(I32), x_scales[0].bitcast(I32))
         nc.sync.dma_start(s_raw[:], sT.rearrange("(p j) v -> p j v", j=PACK))
         nc.sync.dma_start(w2_codes[:].bitcast(I32), words_of(w2_words))
-        load_plane(nc.sync, w2_plane, w2_scales)
-        nc.sync.dma_start(par_sb[:], par)
+        load_plane(nc.sync, w2_plane, w2_scales, range(4))
         nc.sync.dma_start(xw_table[:].bitcast(I32), words_of(x_words))
         nc.sync.dma_start(w1_codes[:].bitcast(I32), words_of(w1_words))
-        load_plane(nc.gpsimd, w1_plane, w1_scales)
+        load_plane(nc.sync, w1_plane, w1_scales, range(2))
 
         def entries(lst, a, b):
             return lst[:, a // STRIPE : b // STRIPE]
@@ -83,28 +84,28 @@ def tile_picked_fpn_relu_p_kernel(
                 s_raw[:, :, a:b].rearrange("p t (c i) -> p c t i", i=4),
             )
 
-        interleave(nc.scalar.copy, 0, SCALAR_COLS)
+        interleave(nc.scalar.copy, 0, V // 4)
+        interleave(nc.scalar.copy, V // 4, SCALAR_COLS)
         interleave(nc.vector.tensor_copy, V // 2, V)
         interleave(nc.vector.tensor_copy, SCALAR_COLS, V // 2)
 
         t_table = keep.tile([P, V], F32, name="t_table", align_bytes=64)
-        for h in (1, 0):
-            cols = slice(h * V // 2, (h + 1) * V // 2)
-            s_codes = keep.tile([P, V // 2], U32, name="s_codes%d" % h, align_bytes=64)
-            s_plane = keep.tile([P, V // 2], U8, name="s_plane%d" % h, align_bytes=64)
-            nc.vector.quantize_mx(s_codes[:].bitcast(FP8X4), s_plane[:], s_grouped[:, PACK * cols.start : PACK * cols.stop])
-            t_bank = psum.tile([P, V // 2], F32, name="t_bank%d" % h)
+        for a, b in ((V // 2, V), (0, V // 4), (V // 4, V // 2)):
+            s_codes = keep.tile([P, b - a], U32, name="s_codes%d" % a, align_bytes=64)
+            s_plane = keep.tile([P, b - a], U8, name="s_plane%d" % a, align_bytes=64)
+            nc.vector.quantize_mx(s_codes[:].bitcast(FP8X4), s_plane[:], s_grouped[:, PACK * a : PACK * b])
+            t_bank = psum.tile([P, b - a], F32, name="t_bank%d" % a)
             nc.tensor.matmul_mx(t_bank[:], lhsT=w2_codes[:].bitcast(FP8X4), lhsT_scale=w2_plane[:],
                                 rhs=s_codes[:].bitcast(FP8X4), rhs_scale=s_plane[:], start=True, stop=True)
-            nc.scalar.copy(t_table[:, cols], t_bank[:])
+            nc.scalar.copy(t_table[:, a:b], t_bank[:])
 
         nc.vector.tensor_copy(xs_picked[:, HALF:S], xs_table[:].indirect(entries(offs_sb, HALF, S)))
         for r in range(4):
             nc.sync.dma_start(xs_plane[32 * r : 32 * r + 4, :].bitcast(I32), xs_picked[ROW0 + 4 * r : ROW0 + 4 * r + 4, :].bitcast(I32))
 
         t_picked = keep.tile([P, S], F32, name="t_picked", align_bytes=64)
-        for a in range(0, S, 256):
-            nc.vector.tensor_copy(t_picked[:, a : a + 256], t_table[:].indirect(entries(par_sb, a, a + 256)))
+        for a, b in ((0, 352), (352, 704), (704, S)):
+            nc.vector.tensor_copy(t_picked[:, a:b], t_table[:].indirect(entries(par_sb, a, b)))
 
         xw_picked = []
         for h in range(2):
@@ -112,7 +113,7 @@ def tile_picked_fpn_relu_p_kernel(
             nc.vector.tensor_copy(picked[:], xw_table[:].indirect(entries(offs_sb, h * HALF, (h + 1) * HALF)))
             xw_picked.append(picked)
 
-        for a, b in ((0, 512), (512, 768), (768, 1024)):
+        for a, b in ((0, 256), (256, 512), (512, 768), (768, 1024)):
             h = a // HALF
             y_bank = psum.tile([P, b - a], F32, name="y_bank%d" % a)
             nc.tensor.matmul_mx(y_bank[:], lhsT=w1_codes[:].bitcast(FP8X4), lhsT_scale=w1_plane[:],

@@ -19,8 +19,9 @@ P = 128
 PACK = 4
 STRIPE = 16
 HALF = S // 2
-SCALAR_COLS = 224
+SCALAR_COLS = 320
 ROW0 = P - 16
+X_HEAD = 768
 
 
 def words_of(packed):
@@ -39,7 +40,7 @@ def tile_picked_fpn_relu_p_kernel(
         par_sb = keep.tile([P, S // STRIPE], U16, name="par_sb")
         xs_table = keep.tile([P, T], U8, name="xs_table", align_bytes=64)
         xw_table = keep.tile([P, T], U32, name="xw_table", align_bytes=64)
-        s_raw = keep.tile([P, PACK, V], F32, name="s_raw", align_bytes=64)
+        s_raw = [keep.tile([P, PACK, V // 2], F32, name="s_raw%d" % h, align_bytes=64) for h in range(2)]
         w1_codes = keep.tile([P, N], U32, name="w1_codes", align_bytes=64)
         w2_codes = keep.tile([P, N], U32, name="w2_codes", align_bytes=64)
         w1_plane = keep.tile([P, N], U8, name="w1_plane", align_bytes=64)
@@ -60,13 +61,17 @@ def tile_picked_fpn_relu_p_kernel(
                 queue.dma_start(plane[32 * q : 32 * q + 4, :].bitcast(I32), rows[0, 4 * q : 4 * q + 4, :].bitcast(I32))
 
         load_plane(nc.gpsimd, w1_plane, w1_scales, range(2, 4))
+        s_rows = sT.rearrange("(p j) v -> p j v", j=PACK)
         nc.sync.dma_start(offs_sb[:], offs)
-        nc.sync.dma_start(par_sb[:], par)
         nc.sync.dma_start(xs_table[ROW0:P, :].bitcast(I32), x_scales[0].bitcast(I32))
-        nc.sync.dma_start(s_raw[:], sT.rearrange("(p j) v -> p j v", j=PACK))
+        load_plane(nc.sync, w2_plane, w2_scales, range(2))
+        nc.sync.dma_start(s_raw[0][:], s_rows[:, :, 0 : V // 2])
+        nc.sync.dma_start(s_raw[1][:], s_rows[:, :, V // 2 : V])
         nc.sync.dma_start(w2_codes[:].bitcast(I32), words_of(w2_words))
-        load_plane(nc.sync, w2_plane, w2_scales, range(4))
-        nc.sync.dma_start(xw_table[:].bitcast(I32), words_of(x_words))
+        nc.sync.dma_start(xw_table[:, 0:X_HEAD].bitcast(I32), words_of(x_words)[:, 0:X_HEAD])
+        load_plane(nc.sync, w2_plane, w2_scales, range(2, 4))
+        nc.sync.dma_start(par_sb[:], par)
+        nc.sync.dma_start(xw_table[:, X_HEAD:T].bitcast(I32), words_of(x_words)[:, X_HEAD:T])
         nc.sync.dma_start(w1_codes[:].bitcast(I32), words_of(w1_words))
         load_plane(nc.sync, w1_plane, w1_scales, range(2))
 
@@ -81,23 +86,23 @@ def tile_picked_fpn_relu_p_kernel(
         def interleave(copy, a, b):
             copy(
                 s_grouped[:, PACK * a : PACK * b].rearrange("p (c i t) -> p c t i", i=4, t=PACK),
-                s_raw[:, :, a:b].rearrange("p t (c i) -> p c t i", i=4),
+                s_raw[a // (V // 2)][:, :, a % (V // 2) : a % (V // 2) + b - a].rearrange("p t (c i) -> p c t i", i=4),
             )
 
-        interleave(nc.scalar.copy, 0, V // 4)
-        interleave(nc.scalar.copy, V // 4, SCALAR_COLS)
-        interleave(nc.vector.tensor_copy, V // 2, V)
-        interleave(nc.vector.tensor_copy, SCALAR_COLS, V // 2)
+        interleave(nc.scalar.copy, 0, V // 2)
+        interleave(nc.scalar.copy, V // 2, SCALAR_COLS)
+        interleave(nc.vector.tensor_copy, SCALAR_COLS, V)
 
         t_table = keep.tile([P, V], F32, name="t_table", align_bytes=64)
-        for a, b in ((V // 2, V), (0, V // 4), (V // 4, V // 2)):
+        for a, b in ((0, V // 2), (3 * V // 4, V), (V // 2, 3 * V // 4)):
             s_codes = keep.tile([P, b - a], U32, name="s_codes%d" % a, align_bytes=64)
             s_plane = keep.tile([P, b - a], U8, name="s_plane%d" % a, align_bytes=64)
             nc.vector.quantize_mx(s_codes[:].bitcast(FP8X4), s_plane[:], s_grouped[:, PACK * a : PACK * b])
             t_bank = psum.tile([P, b - a], F32, name="t_bank%d" % a)
             nc.tensor.matmul_mx(t_bank[:], lhsT=w2_codes[:].bitcast(FP8X4), lhsT_scale=w2_plane[:],
                                 rhs=s_codes[:].bitcast(FP8X4), rhs_scale=s_plane[:], start=True, stop=True)
-            nc.scalar.copy(t_table[:, a:b], t_bank[:])
+            copy = nc.vector.tensor_copy if a == V // 2 else nc.scalar.copy
+            copy(t_table[:, a:b], t_bank[:])
 
         nc.vector.tensor_copy(xs_picked[:, HALF:S], xs_table[:].indirect(entries(offs_sb, HALF, S)))
         for r in range(4):
@@ -113,7 +118,8 @@ def tile_picked_fpn_relu_p_kernel(
             nc.vector.tensor_copy(picked[:], xw_table[:].indirect(entries(offs_sb, h * HALF, (h + 1) * HALF)))
             xw_picked.append(picked)
 
-        for a, b in ((0, 256), (256, 512), (512, 768), (768, 1024)):
+        pieces = ((0, 256), (256, 512), (512, 768), (768, 896), (896, 1024))
+        for a, b in pieces:
             h = a // HALF
             y_bank = psum.tile([P, b - a], F32, name="y_bank%d" % a)
             nc.tensor.matmul_mx(y_bank[:], lhsT=w1_codes[:].bitcast(FP8X4), lhsT_scale=w1_plane[:],
@@ -123,4 +129,5 @@ def tile_picked_fpn_relu_p_kernel(
             nc.vector.tensor_tensor(total[:], y_bank[:], t_picked[:, a:b], ADD)
             result = keep.tile([P, b - a], F32, name="result%d" % a, align_bytes=64)
             nc.scalar.activation(result[:], total[:], RELU)
-            nc.sync.dma_start(out[:, a:b], result[:])
+            queue = nc.scalar if b == S else nc.sync
+            queue.dma_start(out[:, a:b], result[:])

@@ -21,7 +21,7 @@ STRIPE = 16
 HALF = S // 2
 SCALAR_COLS = 320
 ROW0 = P - 16
-X_HEAD = 768
+X_HEAD = 384
 
 
 def words_of(packed):

@@ -19,9 +19,9 @@ P = 128
 PACK = 4
 STRIPE = 16
 HALF = S // 2
-SCALAR_COLS = 320
+SCALAR_COLS = 384
 ROW0 = P - 16
-X_HEAD = 384
+X_HEAD = 256
 
 
 def words_of(packed):
@@ -62,8 +62,8 @@ def tile_picked_fpn_relu_p_kernel(
 
         load_plane(nc.gpsimd, w1_plane, w1_scales, range(2, 4))
         s_rows = sT.rearrange("(p j) v -> p j v", j=PACK)
-        nc.sync.dma_start(offs_sb[:], offs)
         nc.sync.dma_start(xs_table[ROW0:P, :].bitcast(I32), x_scales[0].bitcast(I32))
+        nc.sync.dma_start(offs_sb[:], offs)
         load_plane(nc.sync, w2_plane, w2_scales, range(2))
         nc.sync.dma_start(s_raw[0][:], s_rows[:, :, 0 : V // 2])
         nc.sync.dma_start(s_raw[1][:], s_rows[:, :, V // 2 : V])
@@ -93,12 +93,13 @@ def tile_picked_fpn_relu_p_kernel(
         interleave(nc.scalar.copy, V // 2, SCALAR_COLS)
         interleave(nc.vector.tensor_copy, SCALAR_COLS, V)
 
-        t_table = keep.tile([P, V], F32, name="t_table", align_bytes=64)
-        for a, b in ((0, V // 2), (3 * V // 4, V), (V // 2, 3 * V // 4)):
+        t_table = keep.tile([P, V + STRIPE], F32, name="t_table", align_bytes=64)
+        nc.vector.memset(t_table[:, V:], 0.0)
+        for i, (a, b) in enumerate(((0, V // 2), (3 * V // 4, V), (V // 2, 3 * V // 4))):
             s_codes = keep.tile([P, b - a], U32, name="s_codes%d" % a, align_bytes=64)
             s_plane = keep.tile([P, b - a], U8, name="s_plane%d" % a, align_bytes=64)
             nc.vector.quantize_mx(s_codes[:].bitcast(FP8X4), s_plane[:], s_grouped[:, PACK * a : PACK * b])
-            t_bank = psum.tile([P, b - a], F32, name="t_bank%d" % a)
+            t_bank = psum.tile([P, b - a], F32, name="t_bank%d" % a, tag="bank%d" % i)
             nc.tensor.matmul_mx(t_bank[:], lhsT=w2_codes[:].bitcast(FP8X4), lhsT_scale=w2_plane[:],
                                 rhs=s_codes[:].bitcast(FP8X4), rhs_scale=s_plane[:], start=True, stop=True)
             copy = nc.vector.tensor_copy if a == V // 2 else nc.scalar.copy
@@ -109,7 +110,7 @@ def tile_picked_fpn_relu_p_kernel(
             nc.sync.dma_start(xs_plane[32 * r : 32 * r + 4, :].bitcast(I32), xs_picked[ROW0 + 4 * r : ROW0 + 4 * r + 4, :].bitcast(I32))
 
         t_picked = keep.tile([P, S], F32, name="t_picked", align_bytes=64)
-        for a, b in ((0, 352), (352, 704), (704, S)):
+        for a, b in ((0, HALF), (HALF, S)):
             nc.vector.tensor_copy(t_picked[:, a:b], t_table[:].indirect(entries(par_sb, a, b)))
 
         xw_picked = []
@@ -118,16 +119,20 @@ def tile_picked_fpn_relu_p_kernel(
             nc.vector.tensor_copy(picked[:], xw_table[:].indirect(entries(offs_sb, h * HALF, (h + 1) * HALF)))
             xw_picked.append(picked)
 
-        pieces = ((0, 256), (256, 512), (512, 768), (768, 896), (896, 1024))
-        for a, b in pieces:
+        total = keep.tile([P, S], F32, name="total", align_bytes=64)
+        products = ((0, 256), (256, 512), (512, 640), (640, 768), (768, 896), (896, 1024))
+        for i, (a, b) in enumerate(products):
             h = a // HALF
-            y_bank = psum.tile([P, b - a], F32, name="y_bank%d" % a)
+            y_bank = psum.tile([P, b - a], F32, name="y_bank%d" % a, tag="bank%d" % ((3 + i) % 8))
             nc.tensor.matmul_mx(y_bank[:], lhsT=w1_codes[:].bitcast(FP8X4), lhsT_scale=w1_plane[:],
                                 rhs=xw_picked[h][:, a - h * HALF : b - h * HALF].bitcast(FP8X4),
                                 rhs_scale=xs_plane[:, a:b], start=True, stop=True)
-            total = keep.tile([P, b - a], F32, name="total%d" % a, align_bytes=64)
-            nc.vector.tensor_tensor(total[:], y_bank[:], t_picked[:, a:b], ADD)
+            nc.vector.tensor_tensor(total[:, a:b], y_bank[:], t_picked[:, a:b], ADD)
+        for a, b in ((0, 256), (256, 512), (512, 768), (768, 896), (896, 1024)):
             result = keep.tile([P, b - a], F32, name="result%d" % a, align_bytes=64)
-            nc.scalar.activation(result[:], total[:], RELU)
-            queue = nc.scalar if b == S else nc.sync
+            if b - a == 256:
+                nc.scalar.activation(result[:], total[:, a:b], RELU)
+            else:
+                nc.vector.tensor_scalar_max(result[:], total[:, a:b], 0.0)
+            queue = nc.scalar if a == HALF else nc.sync
             queue.dma_start(out[:, a:b], result[:])

@@ -21,7 +21,7 @@ STRIPE = 16
 HALF = S // 2
 SCALAR_COLS = 384
 ROW0 = P - 16
-X_HEAD = 256
+X_HEAD = 1280
 
 
 def words_of(packed):
@@ -64,13 +64,12 @@ def tile_picked_fpn_relu_p_kernel(
         s_rows = sT.rearrange("(p j) v -> p j v", j=PACK)
         nc.sync.dma_start(xs_table[ROW0:P, :].bitcast(I32), x_scales[0].bitcast(I32))
         nc.sync.dma_start(offs_sb[:], offs)
-        load_plane(nc.sync, w2_plane, w2_scales, range(2))
+        nc.sync.dma_start(par_sb[:], par)
         nc.sync.dma_start(s_raw[0][:], s_rows[:, :, 0 : V // 2])
         nc.sync.dma_start(s_raw[1][:], s_rows[:, :, V // 2 : V])
         nc.sync.dma_start(w2_codes[:].bitcast(I32), words_of(w2_words))
+        load_plane(nc.sync, w2_plane, w2_scales, range(4))
         nc.sync.dma_start(xw_table[:, 0:X_HEAD].bitcast(I32), words_of(x_words)[:, 0:X_HEAD])
-        load_plane(nc.sync, w2_plane, w2_scales, range(2, 4))
-        nc.sync.dma_start(par_sb[:], par)
         nc.sync.dma_start(xw_table[:, X_HEAD:T].bitcast(I32), words_of(x_words)[:, X_HEAD:T])
         nc.sync.dma_start(w1_codes[:].bitcast(I32), words_of(w1_words))
         load_plane(nc.sync, w1_plane, w1_scales, range(2))
@@ -79,7 +78,7 @@ def tile_picked_fpn_relu_p_kernel(
             return lst[:, a // STRIPE : b // STRIPE]
 
         xs_picked = keep.tile([P, S], U8, name="xs_picked", align_bytes=64)
-        nc.vector.tensor_copy(xs_picked[:, 0:HALF], xs_table[:].indirect(entries(offs_sb, 0, HALF)))
+        nc.vector.tensor_copy(xs_picked[:], xs_table[:].indirect(offs_sb[:]))
 
         s_grouped = keep.tile([P, V * PACK], BF16, name="s_grouped", align_bytes=64)
 
@@ -105,7 +104,6 @@ def tile_picked_fpn_relu_p_kernel(
             copy = nc.vector.tensor_copy if a == V // 2 else nc.scalar.copy
             copy(t_table[:, a:b], t_bank[:])
 
-        nc.vector.tensor_copy(xs_picked[:, HALF:S], xs_table[:].indirect(entries(offs_sb, HALF, S)))
         for r in range(4):
             nc.sync.dma_start(xs_plane[32 * r : 32 * r + 4, :].bitcast(I32), xs_picked[ROW0 + 4 * r : ROW0 + 4 * r + 4, :].bitcast(I32))
 

@@ -41,6 +41,7 @@ def tile_picked_fpn_relu_p_kernel(
         xs_table = keep.tile([P, T], U8, name="xs_table", align_bytes=64)
         xw_table = keep.tile([P, T], U32, name="xw_table", align_bytes=64)
         s_raw = [keep.tile([P, PACK, V // 2], F32, name="s_raw%d" % h, align_bytes=64) for h in range(2)]
+        t_table = keep.tile([P, V + STRIPE], F32, name="t_table", align_bytes=64)
         w1_codes = keep.tile([P, N], U32, name="w1_codes", align_bytes=64)
         w2_codes = keep.tile([P, N], U32, name="w2_codes", align_bytes=64)
         w1_plane = keep.tile([P, N], U8, name="w1_plane", align_bytes=64)
@@ -51,10 +52,10 @@ def tile_picked_fpn_relu_p_kernel(
         nc.gpsimd.memset(w2_plane[:].bitcast(I32), 0)
         nc.gpsimd.memset(w1_plane[:].bitcast(I32), 0)
         nc.gpsimd.memset(xs_plane[:].bitcast(I32), 0)
+        nc.gpsimd.memset(t_table[:, V:], 0.0)
 
-        warm = keep.tile([P, 2], F32, name="warm")
-        nc.gpsimd.memset(warm[:, 0:1], 0.0)
-        nc.scalar.activation(warm[:, 1:2], warm[:, 0:1], RELU)
+        warm = keep.tile([P, 1], F32, name="warm")
+        nc.scalar.activation(warm[:], t_table[:, V : V + 1], RELU)
 
         def load_plane(queue, plane, rows, quadrants):
             for q in quadrants:
@@ -64,12 +65,12 @@ def tile_picked_fpn_relu_p_kernel(
         s_rows = sT.rearrange("(p j) v -> p j v", j=PACK)
         nc.sync.dma_start(xs_table[ROW0:P, :].bitcast(I32), x_scales[0].bitcast(I32))
         nc.sync.dma_start(offs_sb[:], offs)
-        nc.sync.dma_start(par_sb[:], par)
+        nc.sync.dma_start(w2_codes[:].bitcast(I32), words_of(w2_words))
         nc.sync.dma_start(s_raw[0][:], s_rows[:, :, 0 : V // 2])
         nc.sync.dma_start(s_raw[1][:], s_rows[:, :, V // 2 : V])
-        nc.sync.dma_start(w2_codes[:].bitcast(I32), words_of(w2_words))
         load_plane(nc.sync, w2_plane, w2_scales, range(4))
         nc.sync.dma_start(xw_table[:, 0:X_HEAD].bitcast(I32), words_of(x_words)[:, 0:X_HEAD])
+        nc.sync.dma_start(par_sb[:], par)
         nc.sync.dma_start(xw_table[:, X_HEAD:T].bitcast(I32), words_of(x_words)[:, X_HEAD:T])
         nc.sync.dma_start(w1_codes[:].bitcast(I32), words_of(w1_words))
         load_plane(nc.sync, w1_plane, w1_scales, range(2))
@@ -88,12 +89,10 @@ def tile_picked_fpn_relu_p_kernel(
                 s_raw[a // (V // 2)][:, :, a % (V // 2) : a % (V // 2) + b - a].rearrange("p t (c i) -> p c t i", i=4),
             )
 
-        interleave(nc.scalar.copy, 0, V // 2)
-        interleave(nc.scalar.copy, V // 2, SCALAR_COLS)
+        for a in range(0, SCALAR_COLS, V // 4):
+            interleave(nc.scalar.copy, a, a + V // 4)
         interleave(nc.vector.tensor_copy, SCALAR_COLS, V)
 
-        t_table = keep.tile([P, V + STRIPE], F32, name="t_table", align_bytes=64)
-        nc.vector.memset(t_table[:, V:], 0.0)
         for i, (a, b) in enumerate(((0, V // 2), (3 * V // 4, V), (V // 2, 3 * V // 4))):
             s_codes = keep.tile([P, b - a], U32, name="s_codes%d" % a, align_bytes=64)
             s_plane = keep.tile([P, b - a], U8, name="s_plane%d" % a, align_bytes=64)
@@ -101,8 +100,7 @@ def tile_picked_fpn_relu_p_kernel(
             t_bank = psum.tile([P, b - a], F32, name="t_bank%d" % a, tag="bank%d" % i)
             nc.tensor.matmul_mx(t_bank[:], lhsT=w2_codes[:].bitcast(FP8X4), lhsT_scale=w2_plane[:],
                                 rhs=s_codes[:].bitcast(FP8X4), rhs_scale=s_plane[:], start=True, stop=True)
-            copy = nc.vector.tensor_copy if a == V // 2 else nc.scalar.copy
-            copy(t_table[:, a:b], t_bank[:])
+            nc.scalar.copy(t_table[:, a:b], t_bank[:])
 
         for r in range(4):
             nc.sync.dma_start(xs_plane[32 * r : 32 * r + 4, :].bitcast(I32), xs_picked[ROW0 + 4 * r : ROW0 + 4 * r + 4, :].bitcast(I32))
@@ -118,7 +116,9 @@ def tile_picked_fpn_relu_p_kernel(
             xw_picked.append(picked)
 
         total = keep.tile([P, S], F32, name="total", align_bytes=64)
-        products = ((0, 256), (256, 512), (512, 640), (640, 768), (768, 896), (896, 1024))
+        products = ((0, 128), (128, 256), (256, 512), (512, 640), (640, 768), (768, 896), (896, 1024))
+        relus = ((0, 128), (128, 256), (256, 512), (512, 768), (768, 896), (896, 1024))
+        stores = ((0, 256), (256, 512), (512, 768), (768, 896), (896, 1024))
         for i, (a, b) in enumerate(products):
             h = a // HALF
             y_bank = psum.tile([P, b - a], F32, name="y_bank%d" % a, tag="bank%d" % ((3 + i) % 8))
@@ -126,11 +126,12 @@ def tile_picked_fpn_relu_p_kernel(
                                 rhs=xw_picked[h][:, a - h * HALF : b - h * HALF].bitcast(FP8X4),
                                 rhs_scale=xs_plane[:, a:b], start=True, stop=True)
             nc.vector.tensor_tensor(total[:, a:b], y_bank[:], t_picked[:, a:b], ADD)
-        for a, b in ((0, 256), (256, 512), (512, 768), (768, 896), (896, 1024)):
+        for a, b in stores:
             result = keep.tile([P, b - a], F32, name="result%d" % a, align_bytes=64)
-            if b - a == 256:
-                nc.scalar.activation(result[:], total[:, a:b], RELU)
-            else:
-                nc.vector.tensor_scalar_max(result[:], total[:, a:b], 0.0)
+            for c, d in relus:
+                if a <= c < b and b <= 768:
+                    nc.scalar.activation(result[:, c - a : d - a], total[:, c:d], RELU)
+                elif a <= c < b:
+                    nc.vector.tensor_scalar_max(result[:, c - a : d - a], total[:, c:d], 0.0)
             queue = nc.scalar if a == HALF else nc.sync
             queue.dma_start(out[:, a:b], result[:])

@@ -103,7 +103,7 @@ def tile_picked_fpn_relu_p_kernel(
             nc.scalar.copy(t_table[:, a:b], t_bank[:])
 
         for r in range(4):
-            nc.sync.dma_start(xs_plane[32 * r : 32 * r + 4, :].bitcast(I32), xs_picked[ROW0 + 4 * r : ROW0 + 4 * r + 4, :].bitcast(I32))
+            nc.sync.dma_start(xs_plane[r:P:32, :].bitcast(I32), xs_picked[ROW0 + r : P : 4, :].bitcast(I32))
 
         t_picked = keep.tile([P, S], F32, name="t_picked", align_bytes=64)
         for a, b in ((0, HALF), (HALF, S)):

@@ -22,6 +22,7 @@ HALF = S // 2
 SCALAR_COLS = 384
 ROW0 = P - 16
 X_HEAD = 1280
+PIECE = 128
 
 
 def words_of(packed):
@@ -116,22 +117,16 @@ def tile_picked_fpn_relu_p_kernel(
             xw_picked.append(picked)
 
         total = keep.tile([P, S], F32, name="total", align_bytes=64)
-        products = ((0, 128), (128, 256), (256, 512), (512, 640), (640, 768), (768, 896), (896, 1024))
-        relus = ((0, 128), (128, 256), (256, 512), (512, 768), (768, 896), (896, 1024))
         stores = ((0, 256), (256, 512), (512, 768), (768, 896), (896, 1024))
-        for i, (a, b) in enumerate(products):
+        for i, a in enumerate(range(0, S, PIECE)):
             h = a // HALF
-            y_bank = psum.tile([P, b - a], F32, name="y_bank%d" % a, tag="bank%d" % ((3 + i) % 8))
+            y_bank = psum.tile([P, PIECE], F32, name="y_bank%d" % a, tag="bank%d" % ((3 + i) % 8))
             nc.tensor.matmul_mx(y_bank[:], lhsT=w1_codes[:].bitcast(FP8X4), lhsT_scale=w1_plane[:],
-                                rhs=xw_picked[h][:, a - h * HALF : b - h * HALF].bitcast(FP8X4),
-                                rhs_scale=xs_plane[:, a:b], start=True, stop=True)
-            nc.vector.tensor_tensor(total[:, a:b], y_bank[:], t_picked[:, a:b], ADD)
+                                rhs=xw_picked[h][:, a - h * HALF : a - h * HALF + PIECE].bitcast(FP8X4),
+                                rhs_scale=xs_plane[:, a : a + PIECE], start=True, stop=True)
+            nc.vector.tensor_tensor(total[:, a : a + PIECE], y_bank[:], t_picked[:, a : a + PIECE], ADD)
         for a, b in stores:
             result = keep.tile([P, b - a], F32, name="result%d" % a, align_bytes=64)
-            for c, d in relus:
-                if a <= c < b and b <= 768:
-                    nc.scalar.activation(result[:, c - a : d - a], total[:, c:d], RELU)
-                elif a <= c < b:
-                    nc.vector.tensor_scalar_max(result[:, c - a : d - a], total[:, c:d], 0.0)
-            queue = nc.scalar if a == HALF else nc.sync
-            queue.dma_start(out[:, a:b], result[:])
+            for c in range(a, b, PIECE):
+                nc.scalar.activation(result[:, c - a : c - a + PIECE], total[:, c : c + PIECE], RELU)
+            nc.sync.dma_start(out[:, a:b], result[:])

@@ -117,7 +117,7 @@ def tile_picked_fpn_relu_p_kernel(
             xw_picked.append(picked)
 
         total = keep.tile([P, S], F32, name="total", align_bytes=64)
-        stores = ((0, 256), (256, 512), (512, 768), (768, 896), (896, 1024))
+        stores = ((0, 128), (128, 384), (384, 640), (640, 896), (896, 1024))
         for i, a in enumerate(range(0, S, PIECE)):
             h = a // HALF
             y_bank = psum.tile([P, PIECE], F32, name="y_bank%d" % a, tag="bank%d" % ((3 + i) % 8))

@@ -14,12 +14,13 @@ U8 = mybir.dt.uint8
 FP8X4 = mybir.dt.float8_e4m3fn_x4
 ADD = mybir.AluOpType.add
 RELU = mybir.ActivationFunctionType.Relu
+COPY = mybir.ActivationFunctionType.Copy
 
 P = 128
 PACK = 4
 STRIPE = 16
 HALF = S // 2
-SCALAR_COLS = 384
+VECTOR_COLS = 320
 ROW0 = P - 16
 X_HEAD = 1280
 PIECE = 128
@@ -41,7 +42,7 @@ def tile_picked_fpn_relu_p_kernel(
         par_sb = keep.tile([P, S // STRIPE], U16, name="par_sb")
         xs_table = keep.tile([P, T], U8, name="xs_table", align_bytes=64)
         xw_table = keep.tile([P, T], U32, name="xw_table", align_bytes=64)
-        s_raw = [keep.tile([P, PACK, V // 2], F32, name="s_raw%d" % h, align_bytes=64) for h in range(2)]
+        s_raw = keep.tile([P, PACK, V], F32, name="s_raw", align_bytes=64)
         t_table = keep.tile([P, V + STRIPE], F32, name="t_table", align_bytes=64)
         w1_codes = keep.tile([P, N], U32, name="w1_codes", align_bytes=64)
         w2_codes = keep.tile([P, N], U32, name="w2_codes", align_bytes=64)
@@ -67,8 +68,7 @@ def tile_picked_fpn_relu_p_kernel(
         nc.sync.dma_start(xs_table[ROW0:P, :].bitcast(I32), x_scales[0].bitcast(I32))
         nc.sync.dma_start(offs_sb[:], offs)
         nc.sync.dma_start(w2_codes[:].bitcast(I32), words_of(w2_words))
-        nc.sync.dma_start(s_raw[0][:], s_rows[:, :, 0 : V // 2])
-        nc.sync.dma_start(s_raw[1][:], s_rows[:, :, V // 2 : V])
+        nc.sync.dma_start(s_raw[:], s_rows)
         load_plane(nc.sync, w2_plane, w2_scales, range(4))
         nc.sync.dma_start(xw_table[:, 0:X_HEAD].bitcast(I32), words_of(x_words)[:, 0:X_HEAD])
         nc.sync.dma_start(par_sb[:], par)
@@ -87,14 +87,14 @@ def tile_picked_fpn_relu_p_kernel(
         def interleave(copy, a, b):
             copy(
                 s_grouped[:, PACK * a : PACK * b].rearrange("p (c i t) -> p c t i", i=4, t=PACK),
-                s_raw[a // (V // 2)][:, :, a % (V // 2) : a % (V // 2) + b - a].rearrange("p t (c i) -> p c t i", i=4),
+                s_raw[:, :, a:b].rearrange("p t (c i) -> p c t i", i=4),
             )
 
-        for a in range(0, SCALAR_COLS, V // 4):
-            interleave(nc.scalar.copy, a, a + V // 4)
-        interleave(nc.vector.tensor_copy, SCALAR_COLS, V)
+        interleave(nc.vector.tensor_copy, 0, V // 2)
+        interleave(nc.vector.tensor_copy, V // 2, VECTOR_COLS)
+        interleave(nc.scalar.copy, VECTOR_COLS, V)
 
-        for i, (a, b) in enumerate(((0, V // 2), (3 * V // 4, V), (V // 2, 3 * V // 4))):
+        for i, (a, b) in enumerate(((0, V // 2), (V // 2, V))):
             s_codes = keep.tile([P, b - a], U32, name="s_codes%d" % a, align_bytes=64)
             s_plane = keep.tile([P, b - a], U8, name="s_plane%d" % a, align_bytes=64)
             nc.vector.quantize_mx(s_codes[:].bitcast(FP8X4), s_plane[:], s_grouped[:, PACK * a : PACK * b])
@@ -108,7 +108,7 @@ def tile_picked_fpn_relu_p_kernel(
 
         t_picked = keep.tile([P, S], F32, name="t_picked", align_bytes=64)
         for a, b in ((0, HALF), (HALF, S)):
-            nc.vector.tensor_copy(t_picked[:, a:b], t_table[:].indirect(entries(par_sb, a, b)))
+            nc.scalar.activation(t_picked[:, a:b], t_table[:].indirect(entries(par_sb, a, b)), COPY)
 
         xw_picked = []
         for h in range(2):

@@ -20,9 +20,8 @@ P = 128
 PACK = 4
 STRIPE = 16
 HALF = S // 2
-VECTOR_COLS = 320
-ROW0 = P - 16
-X_HEAD = 1280
+ROW0 = 32
+X_HEAD = 2048
 PIECE = 128
 
 
@@ -50,7 +49,7 @@ def tile_picked_fpn_relu_p_kernel(
         w2_plane = keep.tile([P, N], U8, name="w2_plane", align_bytes=64)
         xs_plane = keep.tile([P, S], U8, name="xs_plane", align_bytes=64)
 
-        nc.vector.memset(xs_table[0:ROW0, :].bitcast(I32), 0)
+        nc.vector.memset(xs_table[:].bitcast(I32), 0)
         nc.gpsimd.memset(w2_plane[:].bitcast(I32), 0)
         nc.gpsimd.memset(w1_plane[:].bitcast(I32), 0)
         nc.gpsimd.memset(xs_plane[:].bitcast(I32), 0)
@@ -65,13 +64,13 @@ def tile_picked_fpn_relu_p_kernel(
 
         load_plane(nc.gpsimd, w1_plane, w1_scales, range(2, 4))
         s_rows = sT.rearrange("(p j) v -> p j v", j=PACK)
-        nc.sync.dma_start(xs_table[ROW0:P, :].bitcast(I32), x_scales[0].bitcast(I32))
-        nc.sync.dma_start(offs_sb[:], offs)
-        nc.sync.dma_start(w2_codes[:].bitcast(I32), words_of(w2_words))
         nc.sync.dma_start(s_raw[:], s_rows)
-        load_plane(nc.sync, w2_plane, w2_scales, range(4))
-        nc.sync.dma_start(xw_table[:, 0:X_HEAD].bitcast(I32), words_of(x_words)[:, 0:X_HEAD])
+        nc.sync.dma_start(xs_table[ROW0 : ROW0 + 64 : 4, :].bitcast(I32), x_scales[0].bitcast(I32))
+        nc.sync.dma_start(offs_sb[:], offs)
         nc.sync.dma_start(par_sb[:], par)
+        nc.sync.dma_start(xw_table[:, 0:X_HEAD].bitcast(I32), words_of(x_words)[:, 0:X_HEAD])
+        nc.sync.dma_start(w2_codes[:].bitcast(I32), words_of(w2_words))
+        load_plane(nc.sync, w2_plane, w2_scales, range(4))
         nc.sync.dma_start(xw_table[:, X_HEAD:T].bitcast(I32), words_of(x_words)[:, X_HEAD:T])
         nc.sync.dma_start(w1_codes[:].bitcast(I32), words_of(w1_words))
         load_plane(nc.sync, w1_plane, w1_scales, range(2))
@@ -90,12 +89,11 @@ def tile_picked_fpn_relu_p_kernel(
                 s_raw[:, :, a:b].rearrange("p t (c i) -> p c t i", i=4),
             )
 
-        interleave(nc.vector.tensor_copy, 0, V // 2)
-        interleave(nc.vector.tensor_copy, V // 2, VECTOR_COLS)
-        interleave(nc.scalar.copy, VECTOR_COLS, V)
+        interleave(nc.scalar.copy, 0, V // 2)
+        interleave(nc.scalar.copy, V // 2, V)
 
         for i, (a, b) in enumerate(((0, V // 2), (V // 2, V))):
-            s_codes = keep.tile([P, b - a], U32, name="s_codes%d" % a, align_bytes=64)
+            s_codes = keep.tile([P, b - a], U32, name="s_codes%d" % a, tag="xs_table" if i == 0 else "s_codes", align_bytes=64)
             s_plane = keep.tile([P, b - a], U8, name="s_plane%d" % a, align_bytes=64)
             nc.vector.quantize_mx(s_codes[:].bitcast(FP8X4), s_plane[:], s_grouped[:, PACK * a : PACK * b])
             t_bank = psum.tile([P, b - a], F32, name="t_bank%d" % a, tag="bank%d" % i)
@@ -104,7 +102,7 @@ def tile_picked_fpn_relu_p_kernel(
             nc.scalar.copy(t_table[:, a:b], t_bank[:])
 
         for r in range(4):
-            nc.sync.dma_start(xs_plane[r:P:32, :].bitcast(I32), xs_picked[ROW0 + r : P : 4, :].bitcast(I32))
+            nc.sync.dma_start(xs_plane[r:P:32, :].bitcast(I32), xs_picked[ROW0 + 4 * r : ROW0 + 64 : 16, :].bitcast(I32))
 
         t_picked = keep.tile([P, S], F32, name="t_picked", align_bytes=64)
         for a, b in ((0, HALF), (HALF, S)):

@@ -20,8 +20,9 @@ P = 128
 PACK = 4
 STRIPE = 16
 HALF = S // 2
+QUARTER = S // 4
 ROW0 = 32
-X_HEAD = 2048
+X_HEAD = 2560
 PIECE = 128
 
 
@@ -99,7 +100,8 @@ def tile_picked_fpn_relu_p_kernel(
             t_bank = psum.tile([P, b - a], F32, name="t_bank%d" % a, tag="bank%d" % i)
             nc.tensor.matmul_mx(t_bank[:], lhsT=w2_codes[:].bitcast(FP8X4), lhsT_scale=w2_plane[:],
                                 rhs=s_codes[:].bitcast(FP8X4), rhs_scale=s_plane[:], start=True, stop=True)
-            nc.scalar.copy(t_table[:, a:b], t_bank[:])
+            copy = nc.scalar.copy if i == 0 else nc.vector.tensor_copy
+            copy(t_table[:, a:b], t_bank[:])
 
         for r in range(4):
             nc.sync.dma_start(xs_plane[r:P:32, :].bitcast(I32), xs_picked[ROW0 + 4 * r : ROW0 + 64 : 16, :].bitcast(I32))
@@ -108,19 +110,16 @@ def tile_picked_fpn_relu_p_kernel(
         for a, b in ((0, HALF), (HALF, S)):
             nc.scalar.activation(t_picked[:, a:b], t_table[:].indirect(entries(par_sb, a, b)), COPY)
 
-        xw_picked = []
-        for h in range(2):
-            picked = keep.tile([P, HALF], U32, name="xw_picked%d" % h, align_bytes=64)
-            nc.vector.tensor_copy(picked[:], xw_table[:].indirect(entries(offs_sb, h * HALF, (h + 1) * HALF)))
-            xw_picked.append(picked)
+        xw_picked = keep.tile([P, S], U32, name="xw_picked", align_bytes=64)
+        for a, b in ((0, HALF), (HALF, HALF + QUARTER), (HALF + QUARTER, S)):
+            nc.vector.tensor_copy(xw_picked[:, a:b], xw_table[:].indirect(entries(offs_sb, a, b)))
 
         total = keep.tile([P, S], F32, name="total", align_bytes=64)
         stores = ((0, 128), (128, 384), (384, 640), (640, 896), (896, 1024))
         for i, a in enumerate(range(0, S, PIECE)):
-            h = a // HALF
             y_bank = psum.tile([P, PIECE], F32, name="y_bank%d" % a, tag="bank%d" % ((3 + i) % 8))
             nc.tensor.matmul_mx(y_bank[:], lhsT=w1_codes[:].bitcast(FP8X4), lhsT_scale=w1_plane[:],
-                                rhs=xw_picked[h][:, a - h * HALF : a - h * HALF + PIECE].bitcast(FP8X4),
+                                rhs=xw_picked[:, a : a + PIECE].bitcast(FP8X4),
                                 rhs_scale=xs_plane[:, a : a + PIECE], start=True, stop=True)
             nc.vector.tensor_tensor(total[:, a : a + PIECE], y_bank[:], t_picked[:, a : a + PIECE], ADD)
         for a, b in stores:

@@ -21,7 +21,6 @@ PACK = 4
 STRIPE = 16
 HALF = S // 2
 QUARTER = S // 4
-ROW0 = 32
 X_HEAD = 2560
 PIECE = 128
 
@@ -53,7 +52,6 @@ def tile_picked_fpn_relu_p_kernel(
         nc.vector.memset(xs_table[:].bitcast(I32), 0)
         nc.gpsimd.memset(w2_plane[:].bitcast(I32), 0)
         nc.gpsimd.memset(w1_plane[:].bitcast(I32), 0)
-        nc.gpsimd.memset(xs_plane[:].bitcast(I32), 0)
         nc.gpsimd.memset(t_table[:, V:], 0.0)
 
         warm = keep.tile([P, 1], F32, name="warm")
@@ -63,10 +61,9 @@ def tile_picked_fpn_relu_p_kernel(
             for q in quadrants:
                 queue.dma_start(plane[32 * q : 32 * q + 4, :].bitcast(I32), rows[0, 4 * q : 4 * q + 4, :].bitcast(I32))
 
-        load_plane(nc.gpsimd, w1_plane, w1_scales, range(2, 4))
         s_rows = sT.rearrange("(p j) v -> p j v", j=PACK)
         nc.sync.dma_start(s_raw[:], s_rows)
-        nc.sync.dma_start(xs_table[ROW0 : ROW0 + 64 : 4, :].bitcast(I32), x_scales[0].bitcast(I32))
+        nc.sync.dma_start(xs_table[0:P:8, :].bitcast(I32), x_scales[0].bitcast(I32))
         nc.sync.dma_start(offs_sb[:], offs)
         nc.sync.dma_start(par_sb[:], par)
         nc.sync.dma_start(xw_table[:, 0:X_HEAD].bitcast(I32), words_of(x_words)[:, 0:X_HEAD])
@@ -74,13 +71,14 @@ def tile_picked_fpn_relu_p_kernel(
         load_plane(nc.sync, w2_plane, w2_scales, range(4))
         nc.sync.dma_start(xw_table[:, X_HEAD:T].bitcast(I32), words_of(x_words)[:, X_HEAD:T])
         nc.sync.dma_start(w1_codes[:].bitcast(I32), words_of(w1_words))
-        load_plane(nc.sync, w1_plane, w1_scales, range(2))
+        load_plane(nc.sync, w1_plane, w1_scales, range(4))
 
         def entries(lst, a, b):
             return lst[:, a // STRIPE : b // STRIPE]
 
         xs_picked = keep.tile([P, S], U8, name="xs_picked", align_bytes=64)
         nc.vector.tensor_copy(xs_picked[:], xs_table[:].indirect(offs_sb[:]))
+        nc.vector.tensor_copy(xs_plane[:].bitcast(I32), xs_picked[:].bitcast(I32))
 
         s_grouped = keep.tile([P, V * PACK], BF16, name="s_grouped", align_bytes=64)
 
@@ -103,8 +101,8 @@ def tile_picked_fpn_relu_p_kernel(
             copy = nc.scalar.copy if i == 0 else nc.vector.tensor_copy
             copy(t_table[:, a:b], t_bank[:])
 
-        for r in range(4):
-            nc.sync.dma_start(xs_plane[r:P:32, :].bitcast(I32), xs_picked[ROW0 + 4 * r : ROW0 + 64 : 16, :].bitcast(I32))
+        for r in range(1, 4):
+            nc.sync.dma_start(xs_plane[r:P:32, :].bitcast(I32), xs_picked[8 * r : P : 32, :].bitcast(I32))
 
         t_picked = keep.tile([P, S], F32, name="t_picked", align_bytes=64)
         for a, b in ((0, HALF), (HALF, S)):

@@ -69,9 +69,10 @@ def tile_picked_fpn_relu_p_kernel(
         nc.sync.dma_start(xw_table[:, 0:X_HEAD].bitcast(I32), words_of(x_words)[:, 0:X_HEAD])
         nc.sync.dma_start(w2_codes[:].bitcast(I32), words_of(w2_words))
         load_plane(nc.sync, w2_plane, w2_scales, range(4))
+        load_plane(nc.sync, w1_plane, w1_scales, range(1))
         nc.sync.dma_start(xw_table[:, X_HEAD:T].bitcast(I32), words_of(x_words)[:, X_HEAD:T])
         nc.sync.dma_start(w1_codes[:].bitcast(I32), words_of(w1_words))
-        load_plane(nc.sync, w1_plane, w1_scales, range(4))
+        load_plane(nc.sync, w1_plane, w1_scales, range(1, 4))
 
         def entries(lst, a, b):
             return lst[:, a // STRIPE : b // STRIPE]

@@ -21,7 +21,7 @@ PACK = 4
 STRIPE = 16
 HALF = S // 2
 QUARTER = S // 4
-X_HEAD = 2560
+X_HEAD = 2048
 PIECE = 128
 
 
@@ -47,7 +47,6 @@ def tile_picked_fpn_relu_p_kernel(
         w2_codes = keep.tile([P, N], U32, name="w2_codes", align_bytes=64)
         w1_plane = keep.tile([P, N], U8, name="w1_plane", align_bytes=64)
         w2_plane = keep.tile([P, N], U8, name="w2_plane", align_bytes=64)
-        xs_plane = keep.tile([P, S], U8, name="xs_plane", align_bytes=64)
 
         nc.vector.memset(xs_table[:].bitcast(I32), 0)
         nc.gpsimd.memset(w2_plane[:].bitcast(I32), 0)
@@ -79,7 +78,6 @@ def tile_picked_fpn_relu_p_kernel(
 
         xs_picked = keep.tile([P, S], U8, name="xs_picked", align_bytes=64)
         nc.vector.tensor_copy(xs_picked[:], xs_table[:].indirect(offs_sb[:]))
-        nc.vector.tensor_copy(xs_plane[:].bitcast(I32), xs_picked[:].bitcast(I32))
 
         s_grouped = keep.tile([P, V * PACK], BF16, name="s_grouped", align_bytes=64)
 
@@ -102,6 +100,8 @@ def tile_picked_fpn_relu_p_kernel(
             copy = nc.scalar.copy if i == 0 else nc.vector.tensor_copy
             copy(t_table[:, a:b], t_bank[:])
 
+        xs_plane = keep.tile([P, S], U8, name="xs_plane", tag="s_grouped", align_bytes=64)
+        nc.vector.tensor_copy(xs_plane[:].bitcast(I32), xs_picked[:].bitcast(I32))
         for r in range(1, 4):
             nc.sync.dma_start(xs_plane[r:P:32, :].bitcast(I32), xs_picked[8 * r : P : 32, :].bitcast(I32))
 
@@ -114,7 +114,7 @@ def tile_picked_fpn_relu_p_kernel(
             nc.vector.tensor_copy(xw_picked[:, a:b], xw_table[:].indirect(entries(offs_sb, a, b)))
 
         total = keep.tile([P, S], F32, name="total", align_bytes=64)
-        stores = ((0, 128), (128, 384), (384, 640), (640, 896), (896, 1024))
+        stores = ((0, 128), (128, 256), (256, 512), (512, 768), (768, 1024))
         for i, a in enumerate(range(0, S, PIECE)):
             y_bank = psum.tile([P, PIECE], F32, name="y_bank%d" % a, tag="bank%d" % ((3 + i) % 8))
             nc.tensor.matmul_mx(y_bank[:], lhsT=w1_codes[:].bitcast(FP8X4), lhsT_scale=w1_plane[:],

from contextlib import ExitStack

import concourse.mybir as mybir

K, T, S, V, N = 512, 4096, 1024, 512, 128
FLOPS = 2 * K * N * (S + V)

F32 = mybir.dt.float32
BF16 = mybir.dt.bfloat16
I32 = mybir.dt.int32
U32 = mybir.dt.uint32
U16 = mybir.dt.uint16
U8 = mybir.dt.uint8
FP8X4 = mybir.dt.float8_e4m3fn_x4
ADD = mybir.AluOpType.add
RELU = mybir.ActivationFunctionType.Relu
COPY = mybir.ActivationFunctionType.Copy

P = 128
PACK = 4
STRIPE = 16
HALF = S // 2
QUARTER = S // 4
X_HEAD = 2048
PIECE = 128


def words_of(packed):
    return packed[0].rearrange("p n t -> p (n t)").bitcast(I32)


def tile_picked_fpn_relu_p_kernel(
    tc, x_words, x_scales, sT, w1_words, w1_scales, w2_words, w2_scales, offs, par, out
):
    nc = tc.nc
    with ExitStack() as ctx:
        keep = ctx.enter_context(tc.tile_pool(name="keep", bufs=1))
        psum = ctx.enter_context(tc.psum_pool(name="psum", bufs=1))

        offs_sb = keep.tile([P, S // STRIPE], U16, name="offs_sb")
        par_sb = keep.tile([P, S // STRIPE], U16, name="par_sb")
        xs_table = keep.tile([P, T], U8, name="xs_table", align_bytes=64)
        xw_table = keep.tile([P, T], U32, name="xw_table", align_bytes=64)
        s_raw = keep.tile([P, PACK, V], F32, name="s_raw", align_bytes=64)
        t_table = keep.tile([P, V + STRIPE], F32, name="t_table", align_bytes=64)
        w1_codes = keep.tile([P, N], U32, name="w1_codes", align_bytes=64)
        w2_codes = keep.tile([P, N], U32, name="w2_codes", align_bytes=64)
        w1_plane = keep.tile([P, N], U8, name="w1_plane", align_bytes=64)
        w2_plane = keep.tile([P, N], U8, name="w2_plane", align_bytes=64)

        nc.vector.memset(xs_table[:].bitcast(I32), 0)
        nc.gpsimd.memset(w2_plane[:].bitcast(I32), 0)
        nc.gpsimd.memset(w1_plane[:].bitcast(I32), 0)
        nc.gpsimd.memset(t_table[:, V:], 0.0)

        warm = keep.tile([P, 1], F32, name="warm")
        nc.scalar.activation(warm[:], t_table[:, V : V + 1], RELU)

        def load_plane(queue, plane, rows, quadrants):
            for q in quadrants:
                queue.dma_start(plane[32 * q : 32 * q + 4, :].bitcast(I32), rows[0, 4 * q : 4 * q + 4, :].bitcast(I32))

        s_rows = sT.rearrange("(p j) v -> p j v", j=PACK)
        nc.sync.dma_start(s_raw[:], s_rows)
        nc.sync.dma_start(xs_table[0:P:8, :].bitcast(I32), x_scales[0].bitcast(I32))
        nc.sync.dma_start(offs_sb[:], offs)
        nc.sync.dma_start(par_sb[:], par)
        nc.sync.dma_start(xw_table[:, 0:X_HEAD].bitcast(I32), words_of(x_words)[:, 0:X_HEAD])
        nc.sync.dma_start(w2_codes[:].bitcast(I32), words_of(w2_words))
        load_plane(nc.sync, w2_plane, w2_scales, range(4))
        load_plane(nc.sync, w1_plane, w1_scales, range(1))
        nc.sync.dma_start(xw_table[:, X_HEAD:T].bitcast(I32), words_of(x_words)[:, X_HEAD:T])
        nc.sync.dma_start(w1_codes[:].bitcast(I32), words_of(w1_words))
        load_plane(nc.sync, w1_plane, w1_scales, range(1, 4))

        def entries(lst, a, b):
            return lst[:, a // STRIPE : b // STRIPE]

        xs_picked = keep.tile([P, S], U8, name="xs_picked", align_bytes=64)
        nc.vector.tensor_copy(xs_picked[:], xs_table[:].indirect(offs_sb[:]))

        s_grouped = keep.tile([P, V * PACK], BF16, name="s_grouped", align_bytes=64)

        def interleave(copy, a, b):
            copy(
                s_grouped[:, PACK * a : PACK * b].rearrange("p (c i t) -> p c t i", i=4, t=PACK),
                s_raw[:, :, a:b].rearrange("p t (c i) -> p c t i", i=4),
            )

        interleave(nc.scalar.copy, 0, V // 2)
        interleave(nc.scalar.copy, V // 2, V)

        for i, (a, b) in enumerate(((0, V // 2), (V // 2, V))):
            s_codes = keep.tile([P, b - a], U32, name="s_codes%d" % a, tag="xs_table" if i == 0 else "s_codes", align_bytes=64)
            s_plane = keep.tile([P, b - a], U8, name="s_plane%d" % a, align_bytes=64)
            nc.vector.quantize_mx(s_codes[:].bitcast(FP8X4), s_plane[:], s_grouped[:, PACK * a : PACK * b])
            t_bank = psum.tile([P, b - a], F32, name="t_bank%d" % a, tag="bank%d" % i)
            nc.tensor.matmul_mx(t_bank[:], lhsT=w2_codes[:].bitcast(FP8X4), lhsT_scale=w2_plane[:],
                                rhs=s_codes[:].bitcast(FP8X4), rhs_scale=s_plane[:], start=True, stop=True)
            copy = nc.scalar.copy if i == 0 else nc.vector.tensor_copy
            copy(t_table[:, a:b], t_bank[:])

        xs_plane = keep.tile([P, S], U8, name="xs_plane", tag="s_grouped", align_bytes=64)
        nc.vector.tensor_copy(xs_plane[:].bitcast(I32), xs_picked[:].bitcast(I32))
        for r in range(1, 4):
            nc.sync.dma_start(xs_plane[r:P:32, :].bitcast(I32), xs_picked[8 * r : P : 32, :].bitcast(I32))

        t_picked = keep.tile([P, S], F32, name="t_picked", align_bytes=64)
        for a, b in ((0, HALF), (HALF, S)):
            nc.scalar.activation(t_picked[:, a:b], t_table[:].indirect(entries(par_sb, a, b)), COPY)

        xw_picked = keep.tile([P, S], U32, name="xw_picked", align_bytes=64)
        for a, b in ((0, HALF), (HALF, HALF + QUARTER), (HALF + QUARTER, S)):
            nc.vector.tensor_copy(xw_picked[:, a:b], xw_table[:].indirect(entries(offs_sb, a, b)))

        total = keep.tile([P, S], F32, name="total", align_bytes=64)
        stores = ((0, 128), (128, 256), (256, 512), (512, 768), (768, 1024))
        for i, a in enumerate(range(0, S, PIECE)):
            y_bank = psum.tile([P, PIECE], F32, name="y_bank%d" % a, tag="bank%d" % ((3 + i) % 8))
            nc.tensor.matmul_mx(y_bank[:], lhsT=w1_codes[:].bitcast(FP8X4), lhsT_scale=w1_plane[:],
                                rhs=xw_picked[:, a : a + PIECE].bitcast(FP8X4),
                                rhs_scale=xs_plane[:, a : a + PIECE], start=True, stop=True)
            nc.vector.tensor_tensor(total[:, a : a + PIECE], y_bank[:], t_picked[:, a : a + PIECE], ADD)
        for a, b in stores:
            result = keep.tile([P, b - a], F32, name="result%d" % a, align_bytes=64)
            for c in range(a, b, PIECE):
                nc.scalar.activation(result[:, c - a : c - a + PIECE], total[:, c : c + PIECE], RELU)
            nc.sync.dma_start(out[:, a:b], result[:])
